import numpy as np
import ml_dtypes


def mxq(x, axis, fmt="e4m3"):
    dtype, down = {"e4m3": (ml_dtypes.float8_e4m3fn, 7), "e5m2": (ml_dtypes.float8_e5m2, 14)}[fmt]
    v = np.moveaxis(np.asarray(x, np.float32).astype(ml_dtypes.bfloat16).astype(np.float64), axis, -1)
    blocks = v.reshape(v.shape[:-1] + (-1, 32))
    amax = np.abs(blocks).max(-1, keepdims=True)
    byte = np.maximum(np.where(amax > 0, np.frexp(amax)[1] - 1 + 127, 0) - down, 1)
    scale = np.exp2(byte - 127.0)
    codes = (blocks / scale).astype(np.float32).astype(dtype).astype(np.float64)
    return np.moveaxis((codes * scale).reshape(v.shape), -1, axis)


WIDE = False


def mx_kscale(k):
    if not WIDE:
        return np.ones(k)
    levels = np.array([10, -10, 5, -5, 0])
    if k % 512:
        return np.exp2(np.random.permutation(np.resize(levels, k // 32))).repeat(32)
    a = np.empty((k // 512, 16))
    for p in range(k // 512):
        a[p, :8] = np.random.permutation(np.resize(levels, 8))
        for g in range(8):
            far = levels[np.abs(levels - a[p, g]) >= 10]
            a[p, g + 8] = far[np.random.randint(len(far))]
    return np.exp2(a.ravel()).repeat(32)


def f64(x):
    return np.asarray(x).astype(np.float64)


def striped(idx):
    return np.tile(idx.reshape(-1, 16).T, (8, 1)).astype(np.uint16)


def unstriped(offs):
    return offs[:16].T.reshape(-1).astype(np.int64)


E2M1 = np.array([0.0, 0.5, 1.0, 1.5, 2.0, 3.0, 4.0, 6.0, -0.0, -0.5, -1.0, -1.5, -2.0, -3.0, -4.0, -6.0])


def pack_weight(w, fmt):
    k, n = w.shape
    w = f64(np.asarray(w, np.float32).astype(ml_dtypes.bfloat16)).reshape(k // 32, 32, n)
    amax = np.abs(w).max(1)
    if fmt == "e4m3":
        byte = np.frexp(amax)[1] - 1 + 127 - 7
    else:
        mant, ex = np.frexp(amax / 6.0)
        byte = np.where(mant > 0.5, ex, ex - 1) + 127
    byte = np.clip(np.where(amax > 0, byte, 1), 1, 254)
    scaled = (w * np.exp2(127.0 - byte)[:, None, :]).reshape(k, n).astype(np.float32)
    by_word = np.ascontiguousarray(scaled.reshape(k // 512, 128, 4, n).transpose(0, 1, 3, 2))
    if fmt == "e4m3":
        words = by_word.astype(ml_dtypes.float8_e4m3fn).view(np.uint8)
    else:
        c = by_word.astype(ml_dtypes.float4_e2m1fn).view(np.uint8) & 0xF
        words = (c[..., 0::2] | (c[..., 1::2] << 4)).reshape(k // 512, 128, 2 * n)
    return np.ascontiguousarray(words), np.ascontiguousarray(byte.astype(np.uint8).reshape(k // 512, 16, n))


def unpack_weight(words, scales, fmt):
    g, _, n = scales.shape
    words = np.ascontiguousarray(words).reshape(g, 128, n, -1)
    if fmt == "e4m3":
        vals = words.view(ml_dtypes.float8_e4m3fn).astype(np.float64)
    else:
        nib = np.empty((g, 128, n, 4), np.uint8)
        nib[..., 0::2] = words & 0xF
        nib[..., 1::2] = words >> 4
        vals = E2M1[nib]
    vals = vals * np.repeat(np.exp2(scales.astype(np.float64) - 127.0), 8, axis=1)[..., None]
    return vals.transpose(0, 1, 3, 2).reshape(g * 512, n)


def gelu(v):
    return 0.5 * v * (1.0 + np.tanh(np.sqrt(2.0 / np.pi) * (v + 0.044715 * v**3)))


K, KA, KB, H, T, S, T3, S2, P = 1536, 512, 1024, 1024, 4096, 1024, 2048, 512, 512

def setup_inputs():
    n = np.random.standard_normal
    s = mx_kscale(K)[:, None]
    u = mx_kscale(H)[:, None]
    d = {}
    d["tab_words"], d["tab_scales"] = pack_weight(n((K, T)) * s, "e4m3")
    d["offs"] = striped(np.random.permutation(T)[:S])
    d["tab2_words"], d["tab2_scales"] = pack_weight(n((H, T3)) / H ** 0.5 / u, "e4m3")
    d["offs2"] = striped(np.random.permutation(T3)[:S2])
    d["pos1"] = striped(np.random.permutation(S)[:P])
    d["pos2"] = striped(np.random.permutation(S)[:P])
    d["w1"] = (n((KA, H)) / K ** 0.5 / s[:KA] * u.T).astype(np.float32)
    d["w4_words"], d["w4_scales"] = pack_weight(n((KB, H)) / K ** 0.5 / s[KA:] * u.T, "e2m1")
    d["b1"] = (0.6 * n(H) * u[:, 0]).astype(np.float32)
    d["ready"] = np.exp(0.5 * n(S2)).astype(np.float32)
    return d

def reference(tab_words, tab_scales, offs, tab2_words, tab2_scales, offs2, pos1, pos2,
              w1, w4_words, w4_scales, b1, ready):
    v = unpack_weight(tab_words, tab_scales, "e4m3")[:, unstriped(offs)]
    v2 = unpack_weight(tab2_words, tab2_scales, "e4m3")[:, unstriped(offs2)]
    w4 = unpack_weight(w4_words, w4_scales, "e2m1")
    w1q = mxq(f64(w1), 0, "e4m3")
    h = (w1q.T @ v[:KA] + w4.T @ v[KA:]) + f64(b1)[:, None]
    e = v2.T @ mxq(h, 0, "e4m3")
    town = e[:, unstriped(pos1)]
    rural = e[:, unstriped(pos2)]
    return np.maximum(town, rural) * f64(ready)[:, None]

@@ -1,0 +1,269 @@
+from contextlib import ExitStack
+
+import concourse.mybir as mybir
+
+F32 = mybir.dt.float32
+BF16 = mybir.dt.bfloat16
+I32 = mybir.dt.int32
+U32 = mybir.dt.uint32
+U16 = mybir.dt.uint16
+U8 = mybir.dt.uint8
+FP8X4 = mybir.dt.float8_e4m3fn_x4
+FP4X4 = mybir.dt.float4_e2m1fn_x4
+IDENT = mybir.ActivationFunctionType.Identity
+ALU = mybir.AluOpType
+
+P = 128
+T, T3 = 4096, 2048
+S, S2, NP = 1024, 512, 512
+H = 1024
+N = 512
+FLOPS = 2 * 1536 * H * S + 2 * H * S2 * S
+
+
+def tile_list_guide_dog_matching_kernel(
+    tc, tab_words, tab_scales, offs, tab2_words, tab2_scales, offs2, pos1, pos2,
+    w1, w4_words, w4_scales, b1, ready, out,
+):
+    nc = tc.nc
+    with ExitStack() as ctx:
+        keep = ctx.enter_context(tc.tile_pool(name="keep", bufs=1))
+        ring = ctx.enter_context(tc.tile_pool(name="ring", bufs=2))
+        psum = ctx.enter_context(tc.psum_pool(name="psum", bufs=1))
+
+        def kept(name, shape, dtype, after=None):
+            return keep.tile(shape, dtype, name=name, tag=after or name, align_bytes=64)
+
+        offs_t = keep.tile([P, S // 16], U16, name="offs_t")
+        offs2_t = keep.tile([P, S2 // 16], U16, name="offs2_t")
+        pos1_t = keep.tile([P, NP // 16], U16, name="pos1_t")
+        pos2_t = keep.tile([P, NP // 16], U16, name="pos2_t")
+
+        tab_w = [kept(f"tab_w{a}", [P, T], I32) for a in range(3)]
+        tab_s = kept("tab_s", [P, T], U8)
+        tab2_w = [kept(f"tab2_w{a}", [P, T3], I32) for a in range(2)]
+        tab2_s = kept("tab2_s", [P, T3], U8)
+        w4_raw = kept("w4_raw", [P, 2 * 2 * H], U8)
+        w4_sraw = kept("w4_sraw", [P, 2 * H], U8)
+        w1_raw = [kept(f"w1_raw{b}", [P, 4, N], F32) for b in range(2)]
+        bias = kept("bias", [P, 2, 4], F32)
+        ready_t = kept("ready_t", [P, 4], F32)
+        v_s12 = [kept(f"v_s{a}", [P, S], U8) for a in (1, 2)]
+
+        nc.vector.memset(w4_sraw[:].bitcast(I32), 0)
+        nc.vector.memset(tab_s[:].bitcast(I32), 0)
+        nc.vector.memset(tab2_s[:].bitcast(I32), 0)
+        for a in range(2):
+            nc.vector.memset(v_s12[a][:].bitcast(I32), 0)
+
+        def words(src):
+            return src.rearrange("p n t -> p (n t)").bitcast(I32)
+
+        def load_w1(b):
+            nc.sync.dma_start(out=w1_raw[b][:], in_=w1[:, b * N:(b + 1) * N].rearrange("(p j) c -> p j c", j=4))
+
+        nc.sync.dma_start(
+            out=w4_raw[:].bitcast(I32).rearrange("p (a n) -> p a n", a=2),
+            in_=w4_words.bitcast(I32).rearrange("a p n -> p a n"))
+        nc.sync.dma_start(out=tab_w[0][:], in_=words(tab_words[0]))
+        nc.sync.dma_start(offs_t[:], offs)
+        load_w1(0)
+        nc.sync.dma_start(out=tab_w[1][:], in_=words(tab_words[1]))
+        nc.sync.dma_start(offs2_t[:], offs2)
+        nc.sync.dma_start(out=tab_w[2][:], in_=words(tab_words[2]))
+        load_w1(1)
+        nc.sync.dma_start(out=tab2_w[0][:], in_=words(tab2_words[0]))
+        nc.sync.dma_start(out=tab2_w[1][:], in_=words(tab2_words[1]))
+        nc.sync.dma_start(pos1_t[:], pos1)
+        nc.sync.dma_start(pos2_t[:], pos2)
+        with nc.allow_non_contiguous_dma(reason="one readiness value a partition"):
+            nc.sync.dma_start(out=ready_t[:], in_=ready.rearrange("(c p) -> p c", p=P))
+
+        for q in range(4):
+            nc.gpsimd.dma_start(
+                out=w4_sraw[32 * q:32 * q + 4, :].bitcast(I32).rearrange("r (a n) -> r a n", a=2),
+                in_=w4_scales[:, 4 * q:4 * q + 4, :].bitcast(I32).rearrange("a r n -> r a n"))
+        for q in range(4):
+            nc.gpsimd.dma_start(
+                out=tab_s[32 * q + 8:32 * q + 20, :].bitcast(I32),
+                in_=tab_scales[:, 4 * q:4 * q + 4, :].bitcast(I32))
+        nc.gpsimd.dma_start(out=bias[:], in_=b1.rearrange("(b p t) -> p b t", b=2, t=4))
+        for q in range(4):
+            nc.gpsimd.dma_start(
+                out=tab2_s[32 * q:32 * q + 8, :].bitcast(I32),
+                in_=tab2_scales[:, 4 * q:4 * q + 4, :].bitcast(I32))
+
+        w4_c = kept("w4_c", [P, 2 * 2 * H], U8)
+        w4_s = kept("w4_s", [P, 2 * H], U8)
+        nc.vector.tensor_copy(
+            out=w4_c[:].bitcast(U16).rearrange("p (g t m) -> p g t m", t=4, m=P),
+            in_=w4_raw[:].bitcast(U16).rearrange("p (g m t) -> p g t m", t=4, m=P))
+        nc.vector.tensor_copy(
+            out=w4_s[:].rearrange("p (g t m) -> p g t m", t=4, m=P),
+            in_=w4_sraw[:].rearrange("p (g m t) -> p g t m", t=4, m=P))
+
+        w1_bf = [kept("w1_bf0", [P, 4 * N], BF16)]
+        w1_c = [kept(f"w1_c{b}", [P, N], U32) for b in range(2)]
+        w1_s = [kept(f"w1_s{b}", [P, N], U8) for b in range(2)]
+
+        def w1_views(b):
+            return (w1_bf[b][:].rearrange("p (t m j) -> p m t j", t=4, j=4),
+                    w1_raw[b][:].rearrange("p j (m t) -> p m t j", t=4))
+
+        def quant_w1(b):
+            nc.vector.quantize_mx(out=w1_c[b][:].bitcast(FP8X4), scales=w1_s[b][:], in_=w1_bf[b][:])
+
+        v_w = [kept("v_w0", [P, S], U32)]
+        v_s0 = kept("v_s0", [P, S], U8, after="w4_sraw")
+
+        def gather_v(a, half):
+            cols = slice(half * N // 16, (half + 1) * N // 16)
+            nc.vector.tensor_copy(out=v_w[a][:, half * N:(half + 1) * N], in_=tab_w[a][:].bitcast(U32).indirect(offs_t[:, cols]))
+
+        def bank(i):
+            return psum.tile([P, N], F32, name=f"bank{i}", tag=f"bank{i}")
+
+        def h_pass(acc, a, b, t, half, start, stop):
+            cols = slice(half * N, (half + 1) * N)
+            if a == 0:
+                lhs = w1_c[b][:, t * P:(t + 1) * P].bitcast(FP8X4)
+                lhs_s = w1_s[b][:, t * P:(t + 1) * P]
+                rhs_s = v_s0[8:P, cols]
+            else:
+                c0 = (a - 1) * H + b * N + t * P
+                lhs = w4_c[:, 2 * c0:2 * (c0 + P)].bitcast(FP4X4)
+                lhs_s = w4_s[:, c0:c0 + P]
+                rhs_s = v_s12[a - 1][:, cols]
+            nc.tensor.matmul_mx(out=acc[:], lhsT=lhs, lhsT_scale=lhs_s, rhs=v_w[a][:, cols].bitcast(FP8X4),
+                                rhs_scale=rhs_s, start=start, stop=stop)
+
+        o, i = w1_views(0)
+        nc.scalar.activation(out=o, in_=i, func=IDENT)
+        gather_v(0, 0)
+        gather_v(0, 1)
+        nc.vector.tensor_copy(out=v_s0[:], in_=tab_s[:].indirect(offs_t[:]))
+        for a in range(2):
+            nc.gpsimd.dma_start(out=v_s12[a][0:112, :].bitcast(I32),
+                                in_=v_s0[12 + 4 * a:12 + 4 * a + 112, :].bitcast(I32))
+        quant_w1(0)
+
+        acc0 = [[bank(4 * half + t) for t in range(4)] for half in range(2)]
+        for half in range(2):
+            for t in range(4):
+                h_pass(acc0[half][t], 0, 0, t, half, True, False)
+        v_w.append(kept("v_w1", [P, S], U32, after="tab_s"))
+        for half in range(2):
+            gather_v(1, half)
+            for t in range(4):
+                h_pass(acc0[half][t], 1, 0, t, half, False, False)
+        v2_s = kept("v2_s", [P, S2], U8)
+        nc.vector.tensor_copy(out=v2_s[:], in_=tab2_s[:].indirect(offs2_t[:]))
+
+        h_c = [[kept(f"h_c{b}{half}", [P, N], U32) for half in range(2)] for b in range(2)]
+        h_s = [[kept(f"h_s{b}{half}", [P, N], U8) for half in range(2)] for b in range(2)]
+
+        def evict_h(acc, rows, b, t):
+            nc.scalar.activation(out=rows[:, t, :], in_=acc[:], func=IDENT, bias=bias[:, b, t:t + 1])
+
+        def new_rows():
+            return ring.tile([P, 4, N], BF16, name="h_rows", bufs=3, align_bytes=64)
+
+        def weave_h(rows, half):
+            woven = kept("h_woven", [P, 4 * N], BF16, after=f"h_woven{half}")
+            nc.vector.tensor_copy(out=woven[:].rearrange("p (n t) -> p n t", t=4),
+                                  in_=rows[:].rearrange("p t n -> p n t"))
+            return woven
+
+        def quant_h(woven, b, half):
+            nc.vector.quantize_mx(out=h_c[b][half][:].bitcast(FP8X4), scales=h_s[b][half][:], in_=woven[:])
+
+        v_w.append(kept("v_w2", [P, S], U32, after="tab2_s"))
+        rows0 = []
+        for half in range(2):
+            gather_v(2, half)
+            rows = new_rows()
+            for t in range(4):
+                h_pass(acc0[half][t], 2, 0, t, half, False, True)
+                evict_h(acc0[half][t], rows, 0, t)
+            rows0.append(rows)
+
+        w1_bf.append(kept("w1_bf1", [P, 4 * N], BF16, after="tab_w2"))
+        o, i = w1_views(1)
+        nc.vector.tensor_copy(out=o, in_=i)
+        quant_w1(1)
+
+        v2_w = [[None, None], [None, None]]
+
+        def gather_v2(a, g, after):
+            v2_w[a][g] = kept(f"v2_w{a}{g}", [P, 256], U32, after=after)
+            nc.vector.tensor_copy(out=v2_w[a][g][:],
+                                  in_=tab2_w[a][:].bitcast(U32).indirect(offs2_t[:, 16 * g:16 * (g + 1)]))
+
+        acc1 = [bank(t) for t in range(4)]
+        rows10 = new_rows()
+        for a in (1, 2):
+            for t in range(4):
+                h_pass(acc1[t], a, 1, t, 0, a == 1, False)
+        for t in range(4):
+            h_pass(acc1[t], 0, 1, t, 0, False, True)
+            evict_h(acc1[t], rows10, 1, t)
+
+        wv = weave_h(rows0[0], 0)
+        gather_v2(0, 0, "w1_raw1")
+        quant_h(wv, 0, 0)
+        wv = weave_h(rows0[1], 1)
+
+        rows11 = new_rows()
+        for t in range(4):
+            acc = bank(4 + t)
+            for a in (1, 2, 0):
+                h_pass(acc, a, 1, t, 1, a == 1, a == 0)
+            evict_h(acc, rows11, 1, t)
+
+        gather_v2(1, 0, "tab_w2")
+        quant_h(wv, 0, 1)
+        wv = weave_h(rows10, 0)
+        wv2 = weave_h(rows11, 1)
+        quant_h(wv, 1, 0)
+        quant_h(wv2, 1, 1)
+        gather_v2(0, 1, "h_woven0")
+        gather_v2(1, 1, "h_woven1")
+
+        def e_pass(acc, m, b, half):
+            cols = slice((m % 2) * P, (m % 2 + 1) * P)
+            nc.tensor.matmul_mx(
+                out=acc[:], lhsT=v2_w[b][m // 2][:, cols].bitcast(FP8X4),
+                lhsT_scale=v2_s[4 * b:P, m * P:(m + 1) * P],
+                rhs=h_c[b][half][:].bitcast(FP8X4), rhs_scale=h_s[b][half][:],
+                start=(b == 0), stop=(b == 1))
+
+        e = [kept(f"e{m}", [P, S], F32) for m in range(4)]
+        for m in range(4):
+            for half in range(2):
+                acc = bank(4 * half + m)
+                for b in range(2):
+                    e_pass(acc, m, b, half)
+                nc.scalar.activation(out=e[m][:, half * N:(half + 1) * N], in_=acc[:], func=IDENT)
+
+        town = [None] * 4
+        rural = [None] * 4
+
+        def finish(m):
+            best = ring.tile([P, NP], F32, name="best")
+            nc.vector.tensor_tensor(out=best[:], in0=town[m][:], in1=rural[m][:], op=ALU.max)
+            res = ring.tile([P, NP], F32, name="res")
+            if m < 3:
+                nc.scalar.activation(out=res[:], in_=best[:], func=IDENT, scale=ready_t[:, m:m + 1])
+            else:
+                nc.vector.tensor_scalar(out=res[:], in0=best[:], scalar1=ready_t[:, m:m + 1], scalar2=None,
+                                        op0=ALU.mult)
+            nc.sync.dma_start(out=out[m * P:(m + 1) * P, :], in_=res[:])
+
+        for m in range(4):
+            town[m] = ring.tile([P, NP], F32, name="town")
+            nc.vector.tensor_copy(out=town[m][:], in_=e[m][:].indirect(pos1_t[:]))
+            if m > 0:
+                finish(m - 1)
+            rural[m] = ring.tile([P, NP], F32, name="rural")
+            nc.vector.tensor_copy(out=rural[m][:], in_=e[m][:].indirect(pos2_t[:]))
+        finish(3)

@@ -29,30 +29,27 @@ def tile_list_guide_dog_matching_kernel(
     with ExitStack() as ctx:
         keep = ctx.enter_context(tc.tile_pool(name="keep", bufs=1))
         ring = ctx.enter_context(tc.tile_pool(name="ring", bufs=2))
+        reuse = ctx.enter_context(tc.tile_pool(name="reuse", bufs=1))
         psum = ctx.enter_context(tc.psum_pool(name="psum", bufs=1))
 
         def kept(name, shape, dtype, after=None):
             return keep.tile(shape, dtype, name=name, tag=after or name, align_bytes=64)
+
+        def placed(name, shape, dtype, kib):
+            return reuse.tile(shape, dtype, name=name, offset=1024 * kib, align_bytes=64)
 
         offs_t = keep.tile([P, S // 16], U16, name="offs_t")
         offs2_t = keep.tile([P, S2 // 16], U16, name="offs2_t")
         pos1_t = keep.tile([P, NP // 16], U16, name="pos1_t")
         pos2_t = keep.tile([P, NP // 16], U16, name="pos2_t")
 
-        tab_w = [kept(f"tab_w{a}", [P, T], I32) for a in range(3)]
-        tab_s = kept("tab_s", [P, T], U8)
-        tab2_w = [kept(f"tab2_w{a}", [P, T3], I32) for a in range(2)]
-        tab2_s = kept("tab2_s", [P, T3], U8)
-        w4_raw = kept("w4_raw", [P, 2 * 2 * H], U8)
-        w4_sraw = kept("w4_sraw", [P, 2 * H], U8)
-        w1_raw = [kept(f"w1_raw{b}", [P, 4, N], F32) for b in range(2)]
+        tab_w = [kept("tab_w0", [P, T], I32)]
+        tab_s = placed("tab_s", [P, T], U8, 26)
+        w4_raw = placed("w4_raw", [P, 4 * H], U8, 15)
         bias = kept("bias", [P, 2, 4], F32)
-        ready_t = kept("ready_t", [P, 4], F32)
         v_s12 = [kept(f"v_s{a}", [P, S], U8) for a in (1, 2)]
 
-        nc.vector.memset(w4_sraw[:].bitcast(I32), 0)
         nc.vector.memset(tab_s[:].bitcast(I32), 0)
-        nc.vector.memset(tab2_s[:].bitcast(I32), 0)
         for a in range(2):
             nc.vector.memset(v_s12[a][:].bitcast(I32), 0)
 
@@ -65,44 +62,34 @@ def tile_list_guide_dog_matching_kernel(
         nc.sync.dma_start(
             out=w4_raw[:].bitcast(I32).rearrange("p (a n) -> p a n", a=2),
             in_=w4_words.bitcast(I32).rearrange("a p n -> p a n"))
-        nc.sync.dma_start(out=tab_w[0][:], in_=words(tab_words[0]))
         nc.sync.dma_start(offs_t[:], offs)
-        load_w1(0)
-        nc.sync.dma_start(out=tab_w[1][:], in_=words(tab_words[1]))
         nc.sync.dma_start(offs2_t[:], offs2)
-        nc.sync.dma_start(out=tab_w[2][:], in_=words(tab_words[2]))
-        load_w1(1)
-        nc.sync.dma_start(out=tab2_w[0][:], in_=words(tab2_words[0]))
-        nc.sync.dma_start(out=tab2_w[1][:], in_=words(tab2_words[1]))
         nc.sync.dma_start(pos1_t[:], pos1)
         nc.sync.dma_start(pos2_t[:], pos2)
-        with nc.allow_non_contiguous_dma(reason="one readiness value a partition"):
-            nc.sync.dma_start(out=ready_t[:], in_=ready.rearrange("(c p) -> p c", p=P))
-
+        nc.sync.dma_start(out=bias[:], in_=b1.rearrange("(b p t) -> p b t", b=2, t=4))
+        nc.sync.dma_start(out=tab_w[0][:], in_=words(tab_words[0]))
         for q in range(4):
-            nc.gpsimd.dma_start(
-                out=w4_sraw[32 * q:32 * q + 4, :].bitcast(I32).rearrange("r (a n) -> r a n", a=2),
-                in_=w4_scales[:, 4 * q:4 * q + 4, :].bitcast(I32).rearrange("a r n -> r a n"))
-        for q in range(4):
-            nc.gpsimd.dma_start(
+            nc.sync.dma_start(
                 out=tab_s[32 * q + 8:32 * q + 20, :].bitcast(I32),
                 in_=tab_scales[:, 4 * q:4 * q + 4, :].bitcast(I32))
-        nc.gpsimd.dma_start(out=bias[:], in_=b1.rearrange("(b p t) -> p b t", b=2, t=4))
-        for q in range(4):
-            nc.gpsimd.dma_start(
-                out=tab2_s[32 * q:32 * q + 8, :].bitcast(I32),
-                in_=tab2_scales[:, 4 * q:4 * q + 4, :].bitcast(I32))
 
         w4_c = kept("w4_c", [P, 2 * 2 * H], U8)
         w4_s = kept("w4_s", [P, 2 * H], U8)
         nc.vector.tensor_copy(
             out=w4_c[:].bitcast(U16).rearrange("p (g t m) -> p g t m", t=4, m=P),
             in_=w4_raw[:].bitcast(U16).rearrange("p (g m t) -> p g t m", t=4, m=P))
-        nc.vector.tensor_copy(
-            out=w4_s[:].rearrange("p (g t m) -> p g t m", t=4, m=P),
-            in_=w4_sraw[:].rearrange("p (g m t) -> p g t m", t=4, m=P))
+        w1_raw = [placed("w1_raw0", [P, 4, N], F32, 18)]
+        load_w1(0)
+        tab_w.append(placed("tab_w1", [P, T], I32, 0))
+        nc.sync.dma_start(out=tab_w[1][:], in_=words(tab_words[1]))
+        w4_sraw = placed("w4_sraw", [P, 2 * H], U8, 16)
+        nc.vector.memset(w4_sraw[:].bitcast(I32), 0)
+        for q in range(4):
+            nc.sync.dma_start(
+                out=w4_sraw[32 * q:32 * q + 4, :].bitcast(I32).rearrange("r (a n) -> r a n", a=2),
+                in_=w4_scales[:, 4 * q:4 * q + 4, :].bitcast(I32).rearrange("a r n -> r a n"))
 
-        w1_bf = [kept("w1_bf0", [P, 4 * N], BF16)]
+        w1_bf = [kept(f"w1_bf{b}", [P, 4 * N], BF16) for b in range(2)]
         w1_c = [kept(f"w1_c{b}", [P, N], U32) for b in range(2)]
         w1_s = [kept(f"w1_s{b}", [P, N], U8) for b in range(2)]
 
@@ -113,12 +100,16 @@ def tile_list_guide_dog_matching_kernel(
         def quant_w1(b):
             nc.vector.quantize_mx(out=w1_c[b][:].bitcast(FP8X4), scales=w1_s[b][:], in_=w1_bf[b][:])
 
-        v_w = [kept("v_w0", [P, S], U32)]
-        v_s0 = kept("v_s0", [P, S], U8, after="w4_sraw")
+        v_w = [[None, None] for a in range(3)]
+        v_s0 = kept("v_s0", [P, S], U8)
 
         def gather_v(a, half):
             cols = slice(half * N // 16, (half + 1) * N // 16)
-            nc.vector.tensor_copy(out=v_w[a][:, half * N:(half + 1) * N], in_=tab_w[a][:].bitcast(U32).indirect(offs_t[:, cols]))
+            if (a, half) == (0, 1):
+                v_w[a][half] = placed("v_w01", [P, N], U32, 26)
+            else:
+                v_w[a][half] = kept(f"v_w{a}{half}", [P, N], U32)
+            nc.vector.tensor_copy(out=v_w[a][half][:], in_=tab_w[a][:].bitcast(U32).indirect(offs_t[:, cols]))
 
         def bank(i):
             return psum.tile([P, N], F32, name=f"bank{i}", tag=f"bank{i}")
@@ -134,30 +125,46 @@ def tile_list_guide_dog_matching_kernel(
                 lhs = w4_c[:, 2 * c0:2 * (c0 + P)].bitcast(FP4X4)
                 lhs_s = w4_s[:, c0:c0 + P]
                 rhs_s = v_s12[a - 1][:, cols]
-            nc.tensor.matmul_mx(out=acc[:], lhsT=lhs, lhsT_scale=lhs_s, rhs=v_w[a][:, cols].bitcast(FP8X4),
+            nc.tensor.matmul_mx(out=acc[:], lhsT=lhs, lhsT_scale=lhs_s, rhs=v_w[a][half][:].bitcast(FP8X4),
                                 rhs_scale=rhs_s, start=start, stop=stop)
 
         o, i = w1_views(0)
         nc.scalar.activation(out=o, in_=i, func=IDENT)
         gather_v(0, 0)
-        gather_v(0, 1)
         nc.vector.tensor_copy(out=v_s0[:], in_=tab_s[:].indirect(offs_t[:]))
         for a in range(2):
-            nc.gpsimd.dma_start(out=v_s12[a][0:112, :].bitcast(I32),
-                                in_=v_s0[12 + 4 * a:12 + 4 * a + 112, :].bitcast(I32))
+            nc.sync.dma_start(out=v_s12[a][0:112, :].bitcast(I32),
+                              in_=v_s0[12 + 4 * a:12 + 4 * a + 112, :].bitcast(I32))
+        tab_w.append(placed("tab_w2", [P, T], I32, 28))
+        nc.sync.dma_start(out=tab_w[2][:], in_=words(tab_words[2]))
+        gather_v(0, 1)
         quant_w1(0)
+        w1_raw.append(kept("w1_raw1", [P, 4, N], F32, after="w1_bf0"))
+        load_w1(1)
 
         acc0 = [[bank(4 * half + t) for t in range(4)] for half in range(2)]
         for half in range(2):
             for t in range(4):
                 h_pass(acc0[half][t], 0, 0, t, half, True, False)
-        v_w.append(kept("v_w1", [P, S], U32, after="tab_s"))
+        nc.vector.tensor_copy(
+            out=w4_s[:].rearrange("p (g t m) -> p g t m", t=4, m=P),
+            in_=w4_sraw[:].rearrange("p (g m t) -> p g t m", t=4, m=P))
+        tab2_s = placed("tab2_s", [P, T3], U8, 16)
+        nc.vector.memset(tab2_s[:].bitcast(I32), 0)
+        for q in range(4):
+            nc.sync.dma_start(
+                out=tab2_s[32 * q:32 * q + 8, :].bitcast(I32),
+                in_=tab2_scales[:, 4 * q:4 * q + 4, :].bitcast(I32))
         for half in range(2):
             gather_v(1, half)
+        for half in range(2):
             for t in range(4):
                 h_pass(acc0[half][t], 1, 0, t, half, False, False)
-        v2_s = kept("v2_s", [P, S2], U8)
-        nc.vector.tensor_copy(out=v2_s[:], in_=tab2_s[:].indirect(offs2_t[:]))
+        tab2_w = [placed("tab2_w0", [P, T3], I32, 0)]
+        nc.sync.dma_start(out=tab2_w[0][:], in_=words(tab2_words[0]))
+        ready_t = placed("ready_t", [P, 4], F32, 8)
+        with nc.allow_non_contiguous_dma(reason="one readiness value a partition"):
+            nc.sync.dma_start(out=ready_t[:], in_=ready.rearrange("(c p) -> p c", p=P))
 
         h_c = [[kept(f"h_c{b}{half}", [P, N], U32) for half in range(2)] for b in range(2)]
         h_s = [[kept(f"h_s{b}{half}", [P, N], U8) for half in range(2)] for b in range(2)]
@@ -168,16 +175,15 @@ def tile_list_guide_dog_matching_kernel(
         def new_rows():
             return ring.tile([P, 4, N], BF16, name="h_rows", bufs=3, align_bytes=64)
 
-        def weave_h(rows, half):
-            woven = kept("h_woven", [P, 4 * N], BF16, after=f"h_woven{half}")
-            nc.vector.tensor_copy(out=woven[:].rearrange("p (n t) -> p n t", t=4),
-                                  in_=rows[:].rearrange("p t n -> p n t"))
+        def weave_h(rows):
+            woven = ring.tile([P, 4 * N], BF16, name="h_woven", align_bytes=64)
+            nc.vector.tensor_copy(out=woven[:].rearrange("p (c i t) -> p c t i", i=4, t=4),
+                                  in_=rows[:].rearrange("p t (c i) -> p c t i", i=4))
             return woven
 
         def quant_h(woven, b, half):
             nc.vector.quantize_mx(out=h_c[b][half][:].bitcast(FP8X4), scales=h_s[b][half][:], in_=woven[:])
 
-        v_w.append(kept("v_w2", [P, S], U32, after="tab2_s"))
         rows0 = []
         for half in range(2):
             gather_v(2, half)
@@ -187,15 +193,19 @@ def tile_list_guide_dog_matching_kernel(
                 evict_h(acc0[half][t], rows, 0, t)
             rows0.append(rows)
 
-        w1_bf.append(kept("w1_bf1", [P, 4 * N], BF16, after="tab_w2"))
+        tab2_w.append(placed("tab2_w1", [P, T3], I32, 28))
+        nc.sync.dma_start(out=tab2_w[1][:], in_=words(tab2_words[1]))
         o, i = w1_views(1)
         nc.vector.tensor_copy(out=o, in_=i)
         quant_w1(1)
 
         v2_w = [[None, None], [None, None]]
 
-        def gather_v2(a, g, after):
-            v2_w[a][g] = kept(f"v2_w{a}{g}", [P, 256], U32, after=after)
+        def gather_v2(a, g):
+            if g == 0:
+                v2_w[a][g] = kept(f"v2_w{a}", [P, 256], U32)
+            else:
+                v2_w[a][g] = ring.tile([P, 256], U32, name=f"v2_w{a}1", tag="h_woven", align_bytes=64)
             nc.vector.tensor_copy(out=v2_w[a][g][:],
                                   in_=tab2_w[a][:].bitcast(U32).indirect(offs2_t[:, 16 * g:16 * (g + 1)]))
 
@@ -208,10 +218,11 @@ def tile_list_guide_dog_matching_kernel(
             h_pass(acc1[t], 0, 1, t, 0, False, True)
             evict_h(acc1[t], rows10, 1, t)
 
-        wv = weave_h(rows0[0], 0)
-        gather_v2(0, 0, "w1_raw1")
-        quant_h(wv, 0, 0)
-        wv = weave_h(rows0[1], 1)
+        wv0 = weave_h(rows0[0])
+        v2_s = kept("v2_s", [P, S2], U8)
+        nc.vector.tensor_copy(out=v2_s[:], in_=tab2_s[:].indirect(offs2_t[:]))
+        quant_h(wv0, 0, 0)
+        wv = weave_h(rows0[1])
 
         rows11 = new_rows()
         for t in range(4):
@@ -220,14 +231,20 @@ def tile_list_guide_dog_matching_kernel(
                 h_pass(acc, a, 1, t, 1, a == 1, a == 0)
             evict_h(acc, rows11, 1, t)
 
-        gather_v2(1, 0, "tab_w2")
+        gather_v2(0, 0)
         quant_h(wv, 0, 1)
-        wv = weave_h(rows10, 0)
-        wv2 = weave_h(rows11, 1)
+        wv = weave_h(rows10)
+        gather_v2(1, 0)
         quant_h(wv, 1, 0)
+        wv2 = ring.tile([P, 4 * N], BF16, name="h_woven", align_bytes=64)
+        cut = 256
+        nc.scalar.copy(out=wv2[:, :4 * cut].rearrange("p (c i t) -> p c t i", i=4, t=4),
+                       in_=rows11[:, :, :cut].rearrange("p t (c i) -> p c t i", i=4))
+        nc.vector.tensor_copy(out=wv2[:, 4 * cut:].rearrange("p (c i t) -> p c t i", i=4, t=4),
+                              in_=rows11[:, :, cut:].rearrange("p t (c i) -> p c t i", i=4))
+        gather_v2(0, 1)
         quant_h(wv2, 1, 1)
-        gather_v2(0, 1, "h_woven0")
-        gather_v2(1, 1, "h_woven1")
+        gather_v2(1, 1)
 
         def e_pass(acc, m, b, half):
             cols = slice((m % 2) * P, (m % 2 + 1) * P)

@@ -45,7 +45,7 @@ def tile_list_guide_dog_matching_kernel(
 
         tab_w = [kept("tab_w0", [P, T], I32)]
         tab_s = placed("tab_s", [P, T], U8, 26)
-        w4_raw = placed("w4_raw", [P, 4 * H], U8, 15)
+        w4_raw = [placed("w4_raw0", [P, 2 * H], U8, 17), placed("w4_raw1", [P, 2 * H], U8, 14)]
         bias = kept("bias", [P, 2, 4], F32)
         v_s12 = [kept(f"v_s{a}", [P, S], U8) for a in (1, 2)]
 
@@ -59,9 +59,8 @@ def tile_list_guide_dog_matching_kernel(
         def load_w1(b):
             nc.sync.dma_start(out=w1_raw[b][:], in_=w1[:, b * N:(b + 1) * N].rearrange("(p j) c -> p j c", j=4))
 
-        nc.sync.dma_start(
-            out=w4_raw[:].bitcast(I32).rearrange("p (a n) -> p a n", a=2),
-            in_=w4_words.bitcast(I32).rearrange("a p n -> p a n"))
+        for a in range(2):
+            nc.sync.dma_start(out=w4_raw[a][:].bitcast(I32), in_=w4_words[a].bitcast(I32))
         nc.sync.dma_start(offs_t[:], offs)
         nc.sync.dma_start(offs2_t[:], offs2)
         nc.sync.dma_start(pos1_t[:], pos1)
@@ -75,19 +74,24 @@ def tile_list_guide_dog_matching_kernel(
 
         w4_c = kept("w4_c", [P, 2 * 2 * H], U8)
         w4_s = kept("w4_s", [P, 2 * H], U8)
-        nc.vector.tensor_copy(
-            out=w4_c[:].bitcast(U16).rearrange("p (g t m) -> p g t m", t=4, m=P),
-            in_=w4_raw[:].bitcast(U16).rearrange("p (g m t) -> p g t m", t=4, m=P))
+
+        def deal_w4_words(a):
+            nc.vector.tensor_copy(
+                out=w4_c[:, 2 * H * a:2 * H * (a + 1)].bitcast(U16).rearrange("p (g t m) -> p g t m", t=4, m=P),
+                in_=w4_raw[a][:].bitcast(U16).rearrange("p (g m t) -> p g t m", t=4, m=P))
+
+        deal_w4_words(0)
         w1_raw = [placed("w1_raw0", [P, 4, N], F32, 18)]
         load_w1(0)
-        tab_w.append(placed("tab_w1", [P, T], I32, 0))
-        nc.sync.dma_start(out=tab_w[1][:], in_=words(tab_words[1]))
         w4_sraw = placed("w4_sraw", [P, 2 * H], U8, 16)
         nc.vector.memset(w4_sraw[:].bitcast(I32), 0)
         for q in range(4):
             nc.sync.dma_start(
                 out=w4_sraw[32 * q:32 * q + 4, :].bitcast(I32).rearrange("r (a n) -> r a n", a=2),
                 in_=w4_scales[:, 4 * q:4 * q + 4, :].bitcast(I32).rearrange("a r n -> r a n"))
+        deal_w4_words(1)
+        tab_w.append(placed("tab_w1", [P, T], I32, 0))
+        nc.sync.dma_start(out=tab_w[1][:], in_=words(tab_words[1]))
 
         w1_bf = [kept(f"w1_bf{b}", [P, 4 * N], BF16) for b in range(2)]
         w1_c = [kept(f"w1_c{b}", [P, N], U32) for b in range(2)]
@@ -224,7 +228,7 @@ def tile_list_guide_dog_matching_kernel(
         quant_h(wv0, 0, 0)
         wv = weave_h(rows0[1])
 
-        rows11 = new_rows()
+        rows11 = placed("h_rows_last", [P, 4, N], BF16, 44)
         for t in range(4):
             acc = bank(4 + t)
             for a in (1, 2, 0):
@@ -242,45 +246,58 @@ def tile_list_guide_dog_matching_kernel(
                        in_=rows11[:, :, :cut].rearrange("p t (c i) -> p c t i", i=4))
         nc.vector.tensor_copy(out=wv2[:, 4 * cut:].rearrange("p (c i t) -> p c t i", i=4, t=4),
                               in_=rows11[:, :, cut:].rearrange("p t (c i) -> p c t i", i=4))
-        gather_v2(0, 1)
-        quant_h(wv2, 1, 1)
+        for lo in (cut, 0):
+            nc.vector.quantize_mx(out=h_c[1][1][:, lo:lo + cut].bitcast(FP8X4), scales=h_s[1][1][:, lo:lo + cut],
+                                  in_=wv2[:, 4 * lo:4 * (lo + cut)])
+            if lo:
+                gather_v2(0, 1)
         gather_v2(1, 1)
 
-        def e_pass(acc, m, b, half):
+        def e_pass(acc, m, b, half, lo, width):
             cols = slice((m % 2) * P, (m % 2 + 1) * P)
             nc.tensor.matmul_mx(
-                out=acc[:], lhsT=v2_w[b][m // 2][:, cols].bitcast(FP8X4),
+                out=acc[:, :width], lhsT=v2_w[b][m // 2][:, cols].bitcast(FP8X4),
                 lhsT_scale=v2_s[4 * b:P, m * P:(m + 1) * P],
-                rhs=h_c[b][half][:].bitcast(FP8X4), rhs_scale=h_s[b][half][:],
+                rhs=h_c[b][half][:, lo:lo + width].bitcast(FP8X4), rhs_scale=h_s[b][half][:, lo:lo + width],
                 start=(b == 0), stop=(b == 1))
 
-        e = [kept(f"e{m}", [P, S], F32) for m in range(4)]
+        e = [placed("e0", [P, S], F32, 44)] + [kept(f"e{m}", [P, S], F32) for m in range(1, 4)]
         for m in range(4):
-            for half in range(2):
-                acc = bank(4 * half + m)
+            pieces = [(m, 0, 0, N), (4 + m, 1, 0, N)]
+            if m == 0:
+                pieces = [(0, 0, 0, N), (4, 1, cut, cut), (1, 1, 0, cut)]
+            if m == 1:
+                pieces = [(4, 0, 0, N), (1, 1, 0, N)]
+            for bk, half, lo, width in pieces:
+                acc = bank(bk)
                 for b in range(2):
-                    e_pass(acc, m, b, half)
-                nc.scalar.activation(out=e[m][:, half * N:(half + 1) * N], in_=acc[:], func=IDENT)
+                    e_pass(acc, m, b, half, lo, width)
+                nc.scalar.activation(out=e[m][:, half * N + lo:half * N + lo + width], in_=acc[:, :width], func=IDENT)
 
-        town = [None] * 4
-        rural = [None] * 4
+        steps = [(0, 0, NP), (1, 0, NP), (2, 0, NP), (3, 0, NP // 2), (3, NP // 2, NP // 2)]
+        picked = []
 
-        def finish(m):
+        def pick(step, pos_t, name):
+            m, lo, width = step
+            got = ring.tile([P, NP], F32, name=name)
+            nc.vector.tensor_copy(out=got[:, :width], in_=e[m][:].indirect(pos_t[:, lo // 16:(lo + width) // 16]))
+            return got
+
+        def finish(step, town, rural):
+            m, lo, width = step
             best = ring.tile([P, NP], F32, name="best")
-            nc.vector.tensor_tensor(out=best[:], in0=town[m][:], in1=rural[m][:], op=ALU.max)
-            res = ring.tile([P, NP], F32, name="res")
-            if m < 3:
-                nc.scalar.activation(out=res[:], in_=best[:], func=IDENT, scale=ready_t[:, m:m + 1])
+            nc.vector.tensor_tensor(out=best[:, :width], in0=town[:, :width], in1=rural[:, :width], op=ALU.max)
+            res = ring.tile([P, NP], F32, name="res", bufs=3)
+            if step != steps[-1]:
+                nc.scalar.activation(out=res[:, :width], in_=best[:, :width], func=IDENT, scale=ready_t[:, m:m + 1])
             else:
-                nc.vector.tensor_scalar(out=res[:], in0=best[:], scalar1=ready_t[:, m:m + 1], scalar2=None,
-                                        op0=ALU.mult)
-            nc.sync.dma_start(out=out[m * P:(m + 1) * P, :], in_=res[:])
+                nc.vector.tensor_scalar(out=res[:, :width], in0=best[:, :width], scalar1=ready_t[:, m:m + 1],
+                                        scalar2=None, op0=ALU.mult)
+            nc.sync.dma_start(out=out[m * P:(m + 1) * P, lo:lo + width], in_=res[:, :width])
 
-        for m in range(4):
-            town[m] = ring.tile([P, NP], F32, name="town")
-            nc.vector.tensor_copy(out=town[m][:], in_=e[m][:].indirect(pos1_t[:]))
-            if m > 0:
-                finish(m - 1)
-            rural[m] = ring.tile([P, NP], F32, name="rural")
-            nc.vector.tensor_copy(out=rural[m][:], in_=e[m][:].indirect(pos2_t[:]))
-        finish(3)
+        for step in steps:
+            town = pick(step, pos1_t, "town")
+            if picked:
+                finish(*picked[-1])
+            picked.append((step, town, pick(step, pos2_t, "rural")))
+        finish(*picked[-1])

@@ -98,8 +98,8 @@ def tile_list_guide_dog_matching_kernel(
         w1_s = [kept(f"w1_s{b}", [P, N], U8) for b in range(2)]
 
         def w1_views(b):
-            return (w1_bf[b][:].rearrange("p (t m j) -> p m t j", t=4, j=4),
-                    w1_raw[b][:].rearrange("p j (m t) -> p m t j", t=4))
+            return (w1_bf[b][:].rearrange("p (t m j) -> p m j t", t=4, j=4),
+                    w1_raw[b][:].rearrange("p j (m t) -> p m j t", t=4))
 
         def quant_w1(b):
             nc.vector.quantize_mx(out=w1_c[b][:].bitcast(FP8X4), scales=w1_s[b][:], in_=w1_bf[b][:])
@@ -209,7 +209,7 @@ def tile_list_guide_dog_matching_kernel(
             if g == 0:
                 v2_w[a][g] = kept(f"v2_w{a}", [P, 256], U32)
             else:
-                v2_w[a][g] = ring.tile([P, 256], U32, name=f"v2_w{a}1", tag="h_woven", align_bytes=64)
+                v2_w[a][g] = placed(f"v2_w{a}1", [P, 256], U32, 48 + a)
             nc.vector.tensor_copy(out=v2_w[a][g][:],
                                   in_=tab2_w[a][:].bitcast(U32).indirect(offs2_t[:, 16 * g:16 * (g + 1)]))
 
@@ -240,7 +240,7 @@ def tile_list_guide_dog_matching_kernel(
         wv = weave_h(rows10)
         gather_v2(1, 0)
         quant_h(wv, 1, 0)
-        wv2 = ring.tile([P, 4 * N], BF16, name="h_woven", align_bytes=64)
+        wv2 = placed("h_woven_last", [P, 4 * N], BF16, 48)
         cut = 256
         nc.scalar.copy(out=wv2[:, :4 * cut].rearrange("p (c i t) -> p c t i", i=4, t=4),
                        in_=rows11[:, :, :cut].rearrange("p t (c i) -> p c t i", i=4))
@@ -249,8 +249,7 @@ def tile_list_guide_dog_matching_kernel(
         for lo in (cut, 0):
             nc.vector.quantize_mx(out=h_c[1][1][:, lo:lo + cut].bitcast(FP8X4), scales=h_s[1][1][:, lo:lo + cut],
                                   in_=wv2[:, 4 * lo:4 * (lo + cut)])
-            if lo:
-                gather_v2(0, 1)
+        gather_v2(0, 1)
         gather_v2(1, 1)
 
         def e_pass(acc, m, b, half, lo, width):

from contextlib import ExitStack

import concourse.mybir as mybir

F32 = mybir.dt.float32
BF16 = mybir.dt.bfloat16
I32 = mybir.dt.int32
U32 = mybir.dt.uint32
U16 = mybir.dt.uint16
U8 = mybir.dt.uint8
FP8X4 = mybir.dt.float8_e4m3fn_x4
FP4X4 = mybir.dt.float4_e2m1fn_x4
IDENT = mybir.ActivationFunctionType.Identity
ALU = mybir.AluOpType

P = 128
T, T3 = 4096, 2048
S, S2, NP = 1024, 512, 512
H = 1024
N = 512
FLOPS = 2 * 1536 * H * S + 2 * H * S2 * S


def tile_list_guide_dog_matching_kernel(
    tc, tab_words, tab_scales, offs, tab2_words, tab2_scales, offs2, pos1, pos2,
    w1, w4_words, w4_scales, b1, ready, out,
):
    nc = tc.nc
    with ExitStack() as ctx:
        keep = ctx.enter_context(tc.tile_pool(name="keep", bufs=1))
        ring = ctx.enter_context(tc.tile_pool(name="ring", bufs=2))
        reuse = ctx.enter_context(tc.tile_pool(name="reuse", bufs=1))
        psum = ctx.enter_context(tc.psum_pool(name="psum", bufs=1))

        def kept(name, shape, dtype, after=None):
            return keep.tile(shape, dtype, name=name, tag=after or name, align_bytes=64)

        def placed(name, shape, dtype, kib):
            return reuse.tile(shape, dtype, name=name, offset=1024 * kib, align_bytes=64)

        offs_t = keep.tile([P, S // 16], U16, name="offs_t")
        offs2_t = keep.tile([P, S2 // 16], U16, name="offs2_t")
        pos1_t = keep.tile([P, NP // 16], U16, name="pos1_t")
        pos2_t = keep.tile([P, NP // 16], U16, name="pos2_t")

        tab_w = [kept("tab_w0", [P, T], I32)]
        tab_s = placed("tab_s", [P, T], U8, 26)
        w4_raw = [placed("w4_raw0", [P, 2 * H], U8, 17), placed("w4_raw1", [P, 2 * H], U8, 14)]
        bias = kept("bias", [P, 2, 4], F32)
        v_s12 = [kept(f"v_s{a}", [P, S], U8) for a in (1, 2)]

        nc.vector.memset(tab_s[:].bitcast(I32), 0)
        for a in range(2):
            nc.vector.memset(v_s12[a][:].bitcast(I32), 0)

        def words(src):
            return src.rearrange("p n t -> p (n t)").bitcast(I32)

        def load_w1(b):
            nc.sync.dma_start(out=w1_raw[b][:], in_=w1[:, b * N:(b + 1) * N].rearrange("(p j) c -> p j c", j=4))

        for a in range(2):
            nc.sync.dma_start(out=w4_raw[a][:].bitcast(I32), in_=w4_words[a].bitcast(I32))
        nc.sync.dma_start(offs_t[:], offs)
        nc.sync.dma_start(offs2_t[:], offs2)
        nc.sync.dma_start(pos1_t[:], pos1)
        nc.sync.dma_start(pos2_t[:], pos2)
        nc.sync.dma_start(out=bias[:], in_=b1.rearrange("(b p t) -> p b t", b=2, t=4))
        nc.sync.dma_start(out=tab_w[0][:], in_=words(tab_words[0]))
        for q in range(4):
            nc.sync.dma_start(
                out=tab_s[32 * q + 8:32 * q + 20, :].bitcast(I32),
                in_=tab_scales[:, 4 * q:4 * q + 4, :].bitcast(I32))

        w4_c = kept("w4_c", [P, 2 * 2 * H], U8)
        w4_s = kept("w4_s", [P, 2 * H], U8)

        def deal_w4_words(a):
            nc.vector.tensor_copy(
                out=w4_c[:, 2 * H * a:2 * H * (a + 1)].bitcast(U16).rearrange("p (g t m) -> p g t m", t=4, m=P),
                in_=w4_raw[a][:].bitcast(U16).rearrange("p (g m t) -> p g t m", t=4, m=P))

        deal_w4_words(0)
        w1_raw = [placed("w1_raw0", [P, 4, N], F32, 18)]
        load_w1(0)
        w4_sraw = placed("w4_sraw", [P, 2 * H], U8, 16)
        nc.vector.memset(w4_sraw[:].bitcast(I32), 0)
        for q in range(4):
            nc.sync.dma_start(
                out=w4_sraw[32 * q:32 * q + 4, :].bitcast(I32).rearrange("r (a n) -> r a n", a=2),
                in_=w4_scales[:, 4 * q:4 * q + 4, :].bitcast(I32).rearrange("a r n -> r a n"))
        deal_w4_words(1)
        tab_w.append(placed("tab_w1", [P, T], I32, 0))
        nc.sync.dma_start(out=tab_w[1][:], in_=words(tab_words[1]))

        w1_bf = [kept(f"w1_bf{b}", [P, 4 * N], BF16) for b in range(2)]
        w1_c = [kept(f"w1_c{b}", [P, N], U32) for b in range(2)]
        w1_s = [kept(f"w1_s{b}", [P, N], U8) for b in range(2)]

        def w1_views(b):
            return (w1_bf[b][:].rearrange("p (t m j) -> p m j t", t=4, j=4),
                    w1_raw[b][:].rearrange("p j (m t) -> p m j t", t=4))

        def quant_w1(b):
            nc.vector.quantize_mx(out=w1_c[b][:].bitcast(FP8X4), scales=w1_s[b][:], in_=w1_bf[b][:])

        v_w = [[None, None] for a in range(3)]
        v_s0 = kept("v_s0", [P, S], U8)

        def gather_v(a, half):
            cols = slice(half * N // 16, (half + 1) * N // 16)
            if (a, half) == (0, 1):
                v_w[a][half] = placed("v_w01", [P, N], U32, 26)
            else:
                v_w[a][half] = kept(f"v_w{a}{half}", [P, N], U32)
            nc.vector.tensor_copy(out=v_w[a][half][:], in_=tab_w[a][:].bitcast(U32).indirect(offs_t[:, cols]))

        def bank(i):
            return psum.tile([P, N], F32, name=f"bank{i}", tag=f"bank{i}")

        def h_pass(acc, a, b, t, half, start, stop):
            cols = slice(half * N, (half + 1) * N)
            if a == 0:
                lhs = w1_c[b][:, t * P:(t + 1) * P].bitcast(FP8X4)
                lhs_s = w1_s[b][:, t * P:(t + 1) * P]
                rhs_s = v_s0[8:P, cols]
            else:
                c0 = (a - 1) * H + b * N + t * P
                lhs = w4_c[:, 2 * c0:2 * (c0 + P)].bitcast(FP4X4)
                lhs_s = w4_s[:, c0:c0 + P]
                rhs_s = v_s12[a - 1][:, cols]
            nc.tensor.matmul_mx(out=acc[:], lhsT=lhs, lhsT_scale=lhs_s, rhs=v_w[a][half][:].bitcast(FP8X4),
                                rhs_scale=rhs_s, start=start, stop=stop)

        o, i = w1_views(0)
        nc.scalar.activation(out=o, in_=i, func=IDENT)
        gather_v(0, 0)
        nc.vector.tensor_copy(out=v_s0[:], in_=tab_s[:].indirect(offs_t[:]))
        for a in range(2):
            nc.sync.dma_start(out=v_s12[a][0:112, :].bitcast(I32),
                              in_=v_s0[12 + 4 * a:12 + 4 * a + 112, :].bitcast(I32))
        tab_w.append(placed("tab_w2", [P, T], I32, 28))
        nc.sync.dma_start(out=tab_w[2][:], in_=words(tab_words[2]))
        gather_v(0, 1)
        quant_w1(0)
        w1_raw.append(kept("w1_raw1", [P, 4, N], F32, after="w1_bf0"))
        load_w1(1)

        acc0 = [[bank(4 * half + t) for t in range(4)] for half in range(2)]
        for half in range(2):
            for t in range(4):
                h_pass(acc0[half][t], 0, 0, t, half, True, False)
        nc.vector.tensor_copy(
            out=w4_s[:].rearrange("p (g t m) -> p g t m", t=4, m=P),
            in_=w4_sraw[:].rearrange("p (g m t) -> p g t m", t=4, m=P))
        tab2_s = placed("tab2_s", [P, T3], U8, 16)
        nc.vector.memset(tab2_s[:].bitcast(I32), 0)
        for q in range(4):
            nc.sync.dma_start(
                out=tab2_s[32 * q:32 * q + 8, :].bitcast(I32),
                in_=tab2_scales[:, 4 * q:4 * q + 4, :].bitcast(I32))
        for half in range(2):
            gather_v(1, half)
        for half in range(2):
            for t in range(4):
                h_pass(acc0[half][t], 1, 0, t, half, False, False)
        tab2_w = [placed("tab2_w0", [P, T3], I32, 0)]
        nc.sync.dma_start(out=tab2_w[0][:], in_=words(tab2_words[0]))
        ready_t = placed("ready_t", [P, 4], F32, 8)
        with nc.allow_non_contiguous_dma(reason="one readiness value a partition"):
            nc.sync.dma_start(out=ready_t[:], in_=ready.rearrange("(c p) -> p c", p=P))

        h_c = [[kept(f"h_c{b}{half}", [P, N], U32) for half in range(2)] for b in range(2)]
        h_s = [[kept(f"h_s{b}{half}", [P, N], U8) for half in range(2)] for b in range(2)]

        def evict_h(acc, rows, b, t):
            nc.scalar.activation(out=rows[:, t, :], in_=acc[:], func=IDENT, bias=bias[:, b, t:t + 1])

        def new_rows():
            return ring.tile([P, 4, N], BF16, name="h_rows", bufs=3, align_bytes=64)

        def weave_h(rows):
            woven = ring.tile([P, 4 * N], BF16, name="h_woven", align_bytes=64)
            nc.vector.tensor_copy(out=woven[:].rearrange("p (c i t) -> p c t i", i=4, t=4),
                                  in_=rows[:].rearrange("p t (c i) -> p c t i", i=4))
            return woven

        def quant_h(woven, b, half):
            nc.vector.quantize_mx(out=h_c[b][half][:].bitcast(FP8X4), scales=h_s[b][half][:], in_=woven[:])

        rows0 = []
        for half in range(2):
            gather_v(2, half)
            rows = new_rows()
            for t in range(4):
                h_pass(acc0[half][t], 2, 0, t, half, False, True)
                evict_h(acc0[half][t], rows, 0, t)
            rows0.append(rows)

        tab2_w.append(placed("tab2_w1", [P, T3], I32, 28))
        nc.sync.dma_start(out=tab2_w[1][:], in_=words(tab2_words[1]))
        o, i = w1_views(1)
        nc.vector.tensor_copy(out=o, in_=i)
        quant_w1(1)

        v2_w = [[None, None], [None, None]]

        def gather_v2(a, g):
            if g == 0:
                v2_w[a][g] = kept(f"v2_w{a}", [P, 256], U32)
            else:
                v2_w[a][g] = placed(f"v2_w{a}1", [P, 256], U32, 48 + a)
            nc.vector.tensor_copy(out=v2_w[a][g][:],
                                  in_=tab2_w[a][:].bitcast(U32).indirect(offs2_t[:, 16 * g:16 * (g + 1)]))

        acc1 = [bank(t) for t in range(4)]
        rows10 = new_rows()
        for a in (1, 2):
            for t in range(4):
                h_pass(acc1[t], a, 1, t, 0, a == 1, False)
        for t in range(4):
            h_pass(acc1[t], 0, 1, t, 0, False, True)
            evict_h(acc1[t], rows10, 1, t)

        wv0 = weave_h(rows0[0])
        v2_s = kept("v2_s", [P, S2], U8)
        nc.vector.tensor_copy(out=v2_s[:], in_=tab2_s[:].indirect(offs2_t[:]))
        quant_h(wv0, 0, 0)
        wv = weave_h(rows0[1])

        rows11 = placed("h_rows_last", [P, 4, N], BF16, 44)
        for t in range(4):
            acc = bank(4 + t)
            for a in (1, 2, 0):
                h_pass(acc, a, 1, t, 1, a == 1, a == 0)
            evict_h(acc, rows11, 1, t)

        gather_v2(0, 0)
        quant_h(wv, 0, 1)
        wv = weave_h(rows10)
        gather_v2(1, 0)
        quant_h(wv, 1, 0)
        wv2 = placed("h_woven_last", [P, 4 * N], BF16, 48)
        cut = 256
        nc.scalar.copy(out=wv2[:, :4 * cut].rearrange("p (c i t) -> p c t i", i=4, t=4),
                       in_=rows11[:, :, :cut].rearrange("p t (c i) -> p c t i", i=4))
        nc.vector.tensor_copy(out=wv2[:, 4 * cut:].rearrange("p (c i t) -> p c t i", i=4, t=4),
                              in_=rows11[:, :, cut:].rearrange("p t (c i) -> p c t i", i=4))
        for lo in (cut, 0):
            nc.vector.quantize_mx(out=h_c[1][1][:, lo:lo + cut].bitcast(FP8X4), scales=h_s[1][1][:, lo:lo + cut],
                                  in_=wv2[:, 4 * lo:4 * (lo + cut)])
        gather_v2(0, 1)
        gather_v2(1, 1)

        def e_pass(acc, m, b, half, lo, width):
            cols = slice((m % 2) * P, (m % 2 + 1) * P)
            nc.tensor.matmul_mx(
                out=acc[:, :width], lhsT=v2_w[b][m // 2][:, cols].bitcast(FP8X4),
                lhsT_scale=v2_s[4 * b:P, m * P:(m + 1) * P],
                rhs=h_c[b][half][:, lo:lo + width].bitcast(FP8X4), rhs_scale=h_s[b][half][:, lo:lo + width],
                start=(b == 0), stop=(b == 1))

        e = [placed("e0", [P, S], F32, 44)] + [kept(f"e{m}", [P, S], F32) for m in range(1, 4)]
        for m in range(4):
            pieces = [(m, 0, 0, N), (4 + m, 1, 0, N)]
            if m == 0:
                pieces = [(0, 0, 0, N), (4, 1, cut, cut), (1, 1, 0, cut)]
            if m == 1:
                pieces = [(4, 0, 0, N), (1, 1, 0, N)]
            for bk, half, lo, width in pieces:
                acc = bank(bk)
                for b in range(2):
                    e_pass(acc, m, b, half, lo, width)
                nc.scalar.activation(out=e[m][:, half * N + lo:half * N + lo + width], in_=acc[:, :width], func=IDENT)

        steps = [(0, 0, NP), (1, 0, NP), (2, 0, NP), (3, 0, NP // 2), (3, NP // 2, NP // 2)]
        picked = []

        def pick(step, pos_t, name):
            m, lo, width = step
            got = ring.tile([P, NP], F32, name=name)
            nc.vector.tensor_copy(out=got[:, :width], in_=e[m][:].indirect(pos_t[:, lo // 16:(lo + width) // 16]))
            return got

        def finish(step, town, rural):
            m, lo, width = step
            best = ring.tile([P, NP], F32, name="best")
            nc.vector.tensor_tensor(out=best[:, :width], in0=town[:, :width], in1=rural[:, :width], op=ALU.max)
            res = ring.tile([P, NP], F32, name="res", bufs=3)
            if step != steps[-1]:
                nc.scalar.activation(out=res[:, :width], in_=best[:, :width], func=IDENT, scale=ready_t[:, m:m + 1])
            else:
                nc.vector.tensor_scalar(out=res[:, :width], in0=best[:, :width], scalar1=ready_t[:, m:m + 1],
                                        scalar2=None, op0=ALU.mult)
            nc.sync.dma_start(out=out[m * P:(m + 1) * P, lo:lo + width], in_=res[:, :width])

        for step in steps:
            town = pick(step, pos1_t, "town")
            if picked:
                finish(*picked[-1])
            picked.append((step, town, pick(step, pos2_t, "rural")))
        finish(*picked[-1])
